import numpy as np
import ml_dtypes

BF16 = ml_dtypes.bfloat16


def bf(x):
    return np.asarray(x, np.float32).astype(BF16)


def f32(x):
    return np.asarray(x, np.float32)


def f64(x):
    return np.asarray(x).astype(np.float64)


def striped(idx):
    return np.concatenate([l.reshape(-1, 16).T for l in idx])


def rows(idx, k):
    return np.tile(np.repeat(idx, 16, axis=0), (k // (16 * 8), 1))


def look(tab, idx):
    return np.take_along_axis(f64(tab), rows(idx, len(tab)), axis=1)


K, S, D, V, N, M = 512, 2048, 1, 2048, 2048, 128


def setup_inputs():
    return {"tab": f32(0.7 * np.random.standard_normal((D, K, S))), "base": f32(np.random.standard_normal((K, V))), "w": bf(np.random.standard_normal((K, M)) / np.sqrt(K)), "offs": striped(np.random.randint(0, S, (8, N)))}


def reference(tab, base, w, offs):
    idx = np.stack([g.T.reshape(-1) for g in np.split(offs, 8)])
    x = f64(base) + sum(look(tab[d], idx[:, d * V:(d + 1) * V]) for d in range(D))
    y = f64(w).T @ x
    return y

@@ -1,0 +1,54 @@
+import concourse.mybir as mybir
+
+F32, BF16, U16 = mybir.dt.float32, mybir.dt.bfloat16, mybir.dt.uint16
+ADD = mybir.AluOpType.add
+
+P = 128
+PIECE = 512
+FLOPS = 2 * 512 * 128 * 2048 + 512 * 2048
+
+
+def tile_lookup_res_add_none_kernel(tc, tab, base, w, offs, out):
+    nc = tc.nc
+    rows, columns = base.shape
+    words = tab.shape[2]
+    m = w.shape[1]
+    blocks = rows // P
+    pieces = columns // PIECE
+    k = PIECE // 16
+
+    with (
+        tc.tile_pool(name="held", bufs=1) as held,
+        tc.tile_pool(name="ring", bufs=4) as ring,
+        tc.psum_pool(name="psum", bufs=1) as psum,
+    ):
+        offsets = held.tile([P, columns // 16], U16, name="offsets")
+        nc.sync.dma_start(offsets[:], offs)
+        weights = held.tile([P, blocks, m], BF16, name="weights")
+        windows, bases = [], []
+        for r in range(blocks):
+            block = slice(r * P, (r + 1) * P)
+            window = held.tile([P, words], F32, name=f"window{r}")
+            nc.sync.dma_start(window[:], tab[0, block, :])
+            windows.append(window)
+            for p in range(pieces):
+                piece = held.tile([P, PIECE], F32, name=f"base{r}_{p}")
+                nc.sync.dma_start(piece[:], base[block, p * PIECE : (p + 1) * PIECE])
+                bases.append(piece)
+            if r == 0:
+                nc.sync.dma_start(weights[:], w.rearrange("(r p) m -> p r m", p=P))
+
+        banks = [psum.tile([P, PIECE], F32, name=f"bank{p}") for p in range(pieces)]
+        for r in range(blocks):
+            for p in range(pieces):
+                x = ring.tile([P, PIECE], F32, name="x")
+                looked_up = windows[r][:].indirect(offsets[:, p * k : (p + 1) * k])
+                nc.vector.tensor_tensor(x[:], looked_up, bases[r * pieces + p][:], ADD)
+                x_bf16 = ring.tile([P, PIECE], BF16, name="x_bf16")
+                nc.scalar.copy(x_bf16[:], x[:])
+                nc.tensor.matmul(banks[p][:], weights[:, r, :], x_bf16[:], start=r == 0, stop=r == blocks - 1)
+
+        for p in range(pieces):
+            y = ring.tile([P, PIECE], F32, name="y")
+            nc.scalar.copy(y[:], banks[p][:])
+            nc.sync.dma_start(out[:, p * PIECE : (p + 1) * PIECE], y[:])

@@ -19,12 +19,13 @@ def tile_lookup_res_add_none_kernel(tc, tab, base, w, offs, out):
 
     with (
         tc.tile_pool(name="held", bufs=1) as held,
-        tc.tile_pool(name="ring", bufs=4) as ring,
+        tc.tile_pool(name="ring", bufs=8) as ring,
         tc.psum_pool(name="psum", bufs=1) as psum,
     ):
         offsets = held.tile([P, columns // 16], U16, name="offsets")
         nc.sync.dma_start(offsets[:], offs)
         weights = held.tile([P, blocks, m], BF16, name="weights")
+        weights_f32 = held.tile([P, blocks, m], F32, name="weights_f32")
         windows, bases = [], []
         for r in range(blocks):
             block = slice(r * P, (r + 1) * P)
@@ -35,20 +36,28 @@ def tile_lookup_res_add_none_kernel(tc, tab, base, w, offs, out):
                 piece = held.tile([P, PIECE], F32, name=f"base{r}_{p}")
                 nc.sync.dma_start(piece[:], base[block, p * PIECE : (p + 1) * PIECE])
                 bases.append(piece)
-            if r == 0:
-                nc.sync.dma_start(weights[:], w.rearrange("(r p) m -> p r m", p=P))
+                if r == 0 and p == 0:
+                    nc.sync.dma_start(weights[:], w.rearrange("(r p) m -> p r m", p=P))
+                    nc.scalar.copy(weights_f32[:], weights[:])
 
-        banks = [psum.tile([P, PIECE], F32, name=f"bank{p}") for p in range(pieces)]
+        half = PIECE // 2
+        parts = [[slice(0, PIECE)]] * (pieces - 1) + [[slice(0, half), slice(half, PIECE)]]
+        banks = [
+            [psum.tile([P, part.stop - part.start], F32, name=f"bank{p}_{part.start}") for part in parts[p]]
+            for p in range(pieces)
+        ]
         for r in range(blocks):
             for p in range(pieces):
                 x = ring.tile([P, PIECE], F32, name="x")
                 looked_up = windows[r][:].indirect(offsets[:, p * k : (p + 1) * k])
                 nc.vector.tensor_tensor(x[:], looked_up, bases[r * pieces + p][:], ADD)
-                x_bf16 = ring.tile([P, PIECE], BF16, name="x_bf16")
-                nc.scalar.copy(x_bf16[:], x[:])
-                nc.tensor.matmul(banks[p][:], weights[:, r, :], x_bf16[:], start=r == 0, stop=r == blocks - 1)
+                for part, bank in zip(parts[p], banks[p]):
+                    nc.tensor.matmul(bank[:], weights_f32[:, r, :], x[:, part], start=r == 0, stop=r == blocks - 1)
 
         for p in range(pieces):
-            y = ring.tile([P, PIECE], F32, name="y")
-            nc.scalar.copy(y[:], banks[p][:])
-            nc.sync.dma_start(out[:, p * PIECE : (p + 1) * PIECE], y[:])
+            for part, bank in zip(parts[p], banks[p]):
+                y = held.tile([P, part.stop - part.start], F32, name=f"y{p}_{part.start}")
+                vector_is_free = p == pieces - 1 and part.start > 0
+                copy = nc.vector.tensor_copy if vector_is_free else nc.scalar.copy
+                copy(y[:], bank[:])
+                nc.sync.dma_start(out[:, p * PIECE + part.start : p * PIECE + part.stop], y[:])

import concourse.mybir as mybir

F32, BF16, U16 = mybir.dt.float32, mybir.dt.bfloat16, mybir.dt.uint16
ADD = mybir.AluOpType.add

P = 128
PIECE = 512
FLOPS = 2 * 512 * 128 * 2048 + 512 * 2048


def tile_lookup_res_add_none_kernel(tc, tab, base, w, offs, out):
    nc = tc.nc
    rows, columns = base.shape
    words = tab.shape[2]
    m = w.shape[1]
    blocks = rows // P
    pieces = columns // PIECE
    k = PIECE // 16

    with (
        tc.tile_pool(name="held", bufs=1) as held,
        tc.tile_pool(name="ring", bufs=8) as ring,
        tc.psum_pool(name="psum", bufs=1) as psum,
    ):
        offsets = held.tile([P, columns // 16], U16, name="offsets")
        nc.sync.dma_start(offsets[:], offs)
        weights = held.tile([P, blocks, m], BF16, name="weights")
        weights_f32 = held.tile([P, blocks, m], F32, name="weights_f32")
        windows, bases = [], []
        for r in range(blocks):
            block = slice(r * P, (r + 1) * P)
            window = held.tile([P, words], F32, name=f"window{r}")
            nc.sync.dma_start(window[:], tab[0, block, :])
            windows.append(window)
            for p in range(pieces):
                piece = held.tile([P, PIECE], F32, name=f"base{r}_{p}")
                nc.sync.dma_start(piece[:], base[block, p * PIECE : (p + 1) * PIECE])
                bases.append(piece)
                if r == 0 and p == 0:
                    nc.sync.dma_start(weights[:], w.rearrange("(r p) m -> p r m", p=P))
                    nc.scalar.copy(weights_f32[:], weights[:])

        half = PIECE // 2
        parts = [[slice(0, PIECE)]] * (pieces - 1) + [[slice(0, half), slice(half, PIECE)]]
        banks = [
            [psum.tile([P, part.stop - part.start], F32, name=f"bank{p}_{part.start}") for part in parts[p]]
            for p in range(pieces)
        ]
        for r in range(blocks):
            for p in range(pieces):
                x = ring.tile([P, PIECE], F32, name="x")
                looked_up = windows[r][:].indirect(offsets[:, p * k : (p + 1) * k])
                nc.vector.tensor_tensor(x[:], looked_up, bases[r * pieces + p][:], ADD)
                for part, bank in zip(parts[p], banks[p]):
                    nc.tensor.matmul(bank[:], weights_f32[:, r, :], x[:, part], start=r == 0, stop=r == blocks - 1)

        for p in range(pieces):
            for part, bank in zip(parts[p], banks[p]):
                y = held.tile([P, part.stop - part.start], F32, name=f"y{p}_{part.start}")
                vector_is_free = p == pieces - 1 and part.start > 0
                copy = nc.vector.tensor_copy if vector_is_free else nc.scalar.copy
                copy(y[:], bank[:])
                nc.sync.dma_start(out[:, p * PIECE + part.start : p * PIECE + part.stop], y[:])
